import numpy as np
import ml_dtypes


def mxq(x, axis, fmt="e4m3"):
    dtype, down = {"e4m3": (ml_dtypes.float8_e4m3fn, 7), "e5m2": (ml_dtypes.float8_e5m2, 14)}[fmt]
    v = np.moveaxis(np.asarray(x, np.float32).astype(ml_dtypes.bfloat16).astype(np.float64), axis, -1)
    blocks = v.reshape(v.shape[:-1] + (-1, 32))
    amax = np.abs(blocks).max(-1, keepdims=True)
    byte = np.maximum(np.where(amax > 0, np.frexp(amax)[1] - 1 + 127, 0) - down, 1)
    scale = np.exp2(byte - 127.0)
    codes = (blocks / scale).astype(np.float32).astype(dtype).astype(np.float64)
    return np.moveaxis((codes * scale).reshape(v.shape), -1, axis)


WIDE = False


def mx_kscale(k):
    if not WIDE:
        return np.ones(k)
    levels = np.array([10, -10, 5, -5, 0])
    if k % 512:
        return np.exp2(np.random.permutation(np.resize(levels, k // 32))).repeat(32)
    a = np.empty((k // 512, 16))
    for p in range(k // 512):
        a[p, :8] = np.random.permutation(np.resize(levels, 8))
        for g in range(8):
            far = levels[np.abs(levels - a[p, g]) >= 10]
            a[p, g + 8] = far[np.random.randint(len(far))]
    return np.exp2(a.ravel()).repeat(32)


def f64(x):
    return np.asarray(x).astype(np.float64)


def striped(idx):
    return np.tile(idx.reshape(-1, 16).T, (8, 1)).astype(np.uint16)


def unstriped(offs):
    return offs[:16].T.reshape(-1).astype(np.int64)


E2M1 = np.array([0.0, 0.5, 1.0, 1.5, 2.0, 3.0, 4.0, 6.0, -0.0, -0.5, -1.0, -1.5, -2.0, -3.0, -4.0, -6.0])


def pack_weight(w, fmt):
    k, n = w.shape
    w = f64(np.asarray(w, np.float32).astype(ml_dtypes.bfloat16)).reshape(k // 32, 32, n)
    amax = np.abs(w).max(1)
    if fmt == "e4m3":
        byte = np.frexp(amax)[1] - 1 + 127 - 7
    else:
        mant, ex = np.frexp(amax / 6.0)
        byte = np.where(mant > 0.5, ex, ex - 1) + 127
    byte = np.clip(np.where(amax > 0, byte, 1), 1, 254)
    scaled = (w * np.exp2(127.0 - byte)[:, None, :]).reshape(k, n).astype(np.float32)
    by_word = np.ascontiguousarray(scaled.reshape(k // 512, 128, 4, n).transpose(0, 1, 3, 2))
    if fmt == "e4m3":
        words = by_word.astype(ml_dtypes.float8_e4m3fn).view(np.uint8)
    else:
        c = by_word.astype(ml_dtypes.float4_e2m1fn).view(np.uint8) & 0xF
        words = (c[..., 0::2] | (c[..., 1::2] << 4)).reshape(k // 512, 128, 2 * n)
    return np.ascontiguousarray(words), np.ascontiguousarray(byte.astype(np.uint8).reshape(k // 512, 16, n))


def unpack_weight(words, scales, fmt):
    g, _, n = scales.shape
    words = np.ascontiguousarray(words).reshape(g, 128, n, -1)
    if fmt == "e4m3":
        vals = words.view(ml_dtypes.float8_e4m3fn).astype(np.float64)
    else:
        nib = np.empty((g, 128, n, 4), np.uint8)
        nib[..., 0::2] = words & 0xF
        nib[..., 1::2] = words >> 4
        vals = E2M1[nib]
    vals = vals * np.repeat(np.exp2(scales.astype(np.float64) - 127.0), 8, axis=1)[..., None]
    return vals.transpose(0, 1, 3, 2).reshape(g * 512, n)


def gelu(v):
    return 0.5 * v * (1.0 + np.tanh(np.sqrt(2.0 / np.pi) * (v + 0.044715 * v**3)))


K, T, S, S2 = 1024, 2048, 512, 1024

def setup_inputs():
    n = np.random.standard_normal
    s = mx_kscale(K)[:, None]
    d = {}
    d["tab_words"], d["tab_scales"] = pack_weight(n((K, T)) * s, "e4m3")
    d["offs"] = striped(np.random.permutation(T)[:S])
    d["offs2"] = striped(np.random.permutation(T)[:S2])
    d["w1"] = (n((K, K)) / K ** 0.5 / s).astype(np.float32)
    d["w4_words"], d["w4_scales"] = pack_weight(1.5 * n((K, K)) / K ** 0.5 / s, "e2m1")
    d["gain"] = (1.6 * np.exp(0.3 * n(K)) / K ** 0.5 / s[:, 0]).astype(np.float32)
    d["sim"] = (0.9 * n((S2, S))).astype(np.float32)
    return d

def reference(tab_words, tab_scales, offs, offs2, w1, w4_words, w4_scales, gain, sim):
    TW = unpack_weight(tab_words, tab_scales, "e4m3")
    v = TW[:, unstriped(offs)]
    v2 = TW[:, unstriped(offs2)]
    w4 = unpack_weight(w4_words, w4_scales, "e2m1")
    num = mxq(f64(w1), 0, "e4m3").T @ v
    den = w4.T @ v
    h = num / (1.0 + np.abs(den)) * f64(gain)[:, None]
    e = v2.T @ mxq(h, 0, "e4m3")
    return np.maximum(e, f64(sim))

@@ -1,0 +1,226 @@
+from contextlib import ExitStack
+
+import concourse.mybir as mybir
+
+K, T, S, S2 = 1024, 2048, 512, 1024
+FLOPS = 2 * (2 * K * K * S + S2 * K * S)
+
+F32 = mybir.dt.float32
+BF16 = mybir.dt.bfloat16
+I32 = mybir.dt.int32
+U32 = mybir.dt.uint32
+U16 = mybir.dt.uint16
+U8 = mybir.dt.uint8
+FP8X4 = mybir.dt.float8_e4m3fn_x4
+FP4X4 = mybir.dt.float4_e2m1fn_x4
+ACT = mybir.ActivationFunctionType
+ALU = mybir.AluOpType
+
+P = 128
+PACK = 4
+PASS = P * PACK
+PASSES = K // PASS
+QUADS = 4
+JH = 256
+HALVES = S // JH
+PAIR = 2
+
+
+def tile_list_confusable_sign_scores_kernel(
+    tc, tab_words, tab_scales, offs, offs2, w1, w4_words, w4_scales, gain, sim, out
+):
+    nc = tc.nc
+    with ExitStack() as ctx:
+        keep = ctx.enter_context(tc.tile_pool(name="keep", bufs=1))
+        ring = ctx.enter_context(tc.tile_pool(name="ring", bufs=2))
+        outs = ctx.enter_context(tc.tile_pool(name="outs", bufs=8))
+        psum = ctx.enter_context(tc.psum_pool(name="psum", bufs=2))
+        psum_e = ctx.enter_context(tc.psum_pool(name="psum_e", bufs=6))
+
+        def held(shape, dtype, name):
+            return keep.tile(shape, dtype, name=name, align_bytes=64)
+
+        idx = held([P, S // 16], U16, "idx")
+        idx2 = held([P, S2 // 16], U16, "idx2")
+        tab_w = [held([P, T], U32, f"tab_w{a}") for a in range(PASSES)]
+        tab_s = held([P, T], U8, "tab_s")
+        w4_raw = held([P, PASSES, 2 * K], U8, "w4_raw")
+        w4s_raw = held([P, PASSES, K], U8, "w4s_raw")
+        w4_w = [held([P, PASSES, 2 * PASS], U8, f"w4_w{b}") for b in range(PASSES)]
+        w4_s = [held([P, PASSES, PASS], U8, f"w4_s{b}") for b in range(PASSES)]
+        gains = held([P, PASSES, PACK], F32, "gains")
+        w1_raw = {(b, a): held([P, PACK, PASS], F32, f"w1_raw{b}{a}") for b in range(PASSES) for a in range(PASSES)}
+        sims = [held([P, 4, S], F32, f"sims{c}") for c in range(2)]
+        v_w = [held([P, S], U32, f"v_w{a}") for a in range(PASSES)]
+        v_s = held([P, S], U8, "v_s")
+        v_s1 = held([P, S], U8, "v_s1")
+        v2_w = [held([P, S2], U32, f"v2_w{a}") for a in range(PASSES)]
+        v2_s = held([P, S2], U8, "v2_s")
+
+        nc.vector.memset(tab_s[:].bitcast(I32), 0)
+        nc.gpsimd.memset(w4s_raw[:].rearrange("p a c -> p (a c)").bitcast(I32), 0)
+        nc.vector.memset(v_s1[:].bitcast(I32), 0)
+
+        def load_w1(b, a):
+            rows = w1[PASS * a : PASS * (a + 1), PASS * b : PASS * (b + 1)]
+            nc.sync.dma_start(w1_raw[b, a][:], rows.rearrange("(p i) c -> p i c", i=PACK))
+
+        def load_w4_scales(q):
+            nc.sync.dma_start(
+                w4s_raw[32 * q : 32 * q + 4, :, :].bitcast(I32),
+                w4_scales[:, 4 * q : 4 * q + 4, :].rearrange("a r c -> r a c").bitcast(I32),
+            )
+
+        nc.sync.dma_start(idx[:], offs)
+        for q in range(QUADS):
+            nc.sync.dma_start(
+                tab_s[32 * q : 32 * q + 8, :].bitcast(I32), tab_scales[:, 4 * q : 4 * q + 4, :].bitcast(I32)
+            )
+        nc.sync.dma_start(idx2[:], offs2)
+        nc.sync.dma_start(gains[:], gain.rearrange("(b p t) -> p b t", p=P, t=PACK))
+        nc.sync.dma_start(w4_raw[:].bitcast(I32), w4_words.rearrange("a p c -> p a c").bitcast(I32))
+        load_w1(0, 0)
+        for q in range(QUADS):
+            load_w4_scales(q)
+        for a in range(PASSES):
+            nc.sync.dma_start(tab_w[a][:].bitcast(I32), tab_words[a].rearrange("p t i -> p (t i)").bitcast(I32))
+
+        for b in range(PASSES):
+            cols = slice(PASS * b, PASS * (b + 1))
+            nc.scalar.copy(
+                w4_w[b][:].bitcast(U16).rearrange("p a (t m) -> p a t m", t=PACK),
+                w4_raw[:].bitcast(U16)[:, :, cols].rearrange("p a (m t) -> p a t m", t=PACK),
+            )
+            nc.vector.tensor_copy(
+                w4_s[b][:].rearrange("p a (t m) -> p a t m", t=PACK),
+                w4s_raw[:, :, cols].rearrange("p a (m t) -> p a t m", t=PACK),
+            )
+
+        nc.vector.tensor_copy(v_s[:], tab_s[:].indirect(idx[:]))
+        for q in range(QUADS):
+            nc.sync.dma_start(
+                v_s1[32 * q : 32 * q + 4, :].bitcast(I32), v_s[32 * q + 4 : 32 * q + 8, :].bitcast(I32)
+            )
+        for a in range(PASSES):
+            nc.vector.tensor_copy(v_w[a][:], tab_w[a][:].indirect(idx[:]))
+        v_planes = [v_s, v_s1]
+
+        load_w1(0, 1)
+        load_w1(1, 0)
+        load_w1(1, 1)
+        for c in range(2):
+            nc.sync.dma_start(
+                sims[c][:], sim[PASS * c : PASS * (c + 1), :].rearrange("(mt p) j -> p mt j", p=P)
+            )
+
+        w1_w, w1_s, h_w, h_s = {}, {}, {}, {}
+
+        def quantise_w1(b, a):
+            rounded = ring.tile([P, PACK * PASS], BF16, name="w1_bf16", align_bytes=64)
+            dst = rounded[:].rearrange("p (t m i) -> p m i t", t=PACK, i=PACK)
+            src = w1_raw[b, a][:].rearrange("p i (m t) -> p m i t", t=PACK)
+            if (b, a) == (0, 0):
+                nc.scalar.copy(dst, src)
+            else:
+                nc.vector.tensor_copy(dst, src)
+            w1_w[b, a] = held([P, PASS], U32, f"w1_w{b}{a}")
+            w1_s[b, a] = held([P, PASS], U8, f"w1_s{b}{a}")
+            nc.vector.quantize_mx(out=w1_w[b, a][:].bitcast(FP8X4), scales=w1_s[b, a][:], in_=rounded[:])
+
+        pairs = [slice(PAIR * u, PAIR * (u + 1)) for u in range(PACK // PAIR)]
+        size, recip = {}, {}
+
+        def make_size(b, half):
+            js = slice(JH * half, JH * (half + 1))
+            size[b, half] = held([P, PACK, JH], F32, f"size{b}{half}")
+            for ts in pairs:
+                den = psum_e.tile([P, PAIR, JH], F32, name="den", tag="wide")
+                for t in range(ts.start, ts.stop):
+                    for a in range(PASSES):
+                        nc.tensor.matmul_mx(
+                            out=den[:, t - ts.start, :],
+                            lhsT=w4_w[b][:, a, 2 * P * t : 2 * P * (t + 1)].bitcast(FP4X4),
+                            lhsT_scale=w4_s[b][:, a, P * t : P * (t + 1)],
+                            rhs=v_w[a][:, js].bitcast(FP8X4),
+                            rhs_scale=v_planes[a][:, js],
+                            start=(a == 0),
+                            stop=(a == PASSES - 1),
+                        )
+                nc.scalar.activation(size[b, half][:, ts, :], den[:], ACT.Abs)
+
+        def make_recip(b, half):
+            root = ring.tile([P, PACK, JH], F32, name="root")
+            recip[b, half] = held([P, PACK, JH], F32, f"recip{b}{half}")
+            for ts in pairs:
+                nc.scalar.activation(root[:, ts, :], size[b, half][:, ts, :], ACT.Abs_reciprocal_sqrt, bias=1.0)
+            for ts in pairs:
+                nc.scalar.activation(recip[b, half][:, ts, :], root[:, ts, :], ACT.Square)
+
+        def make_h(b, half):
+            js = slice(JH * half, JH * (half + 1))
+            h32 = ring.tile([P, PACK, JH], F32, name="h32")
+            for ts in pairs:
+                num = psum.tile([P, PAIR, JH], F32, name="num")
+                for t in range(ts.start, ts.stop):
+                    for a in range(PASSES):
+                        nc.tensor.matmul_mx(
+                            out=num[:, t - ts.start, :],
+                            lhsT=w1_w[b, a][:, P * t : P * (t + 1)].bitcast(FP8X4),
+                            lhsT_scale=w1_s[b, a][:, P * t : P * (t + 1)],
+                            rhs=v_w[a][:, js].bitcast(FP8X4),
+                            rhs_scale=v_planes[a][:, js],
+                            start=(a == 0),
+                            stop=(a == PASSES - 1),
+                        )
+                for t in range(ts.start, ts.stop):
+                    nc.vector.scalar_tensor_tensor(
+                        h32[:, t, :], num[:, t - ts.start, :], gains[:, b, t : t + 1], recip[b, half][:, t, :],
+                        ALU.mult, ALU.mult,
+                    )
+            rounded = ring.tile([P, JH * PACK], BF16, name="h_bf16", align_bytes=64)
+            nc.vector.tensor_copy(
+                rounded[:].rearrange("p (c i t) -> p c t i", i=4, t=PACK),
+                h32[:].rearrange("p t (c i) -> p c t i", i=4),
+            )
+            h_w[b, half] = held([P, JH], U32, f"h_w{b}{half}")
+            h_s[b, half] = held([P, JH], U8, f"h_s{b}{half}")
+            nc.vector.quantize_mx(out=h_w[b, half][:].bitcast(FP8X4), scales=h_s[b, half][:], in_=rounded[:])
+
+        def score(half):
+            js = slice(JH * half, JH * (half + 1))
+            for mt0 in range(0, S2 // P, PAIR):
+                e = psum_e.tile([P, PAIR, JH], F32, name="e", tag="wide")
+                for mt in range(mt0, mt0 + PAIR):
+                    ms = slice(P * mt, P * (mt + 1))
+                    for b in range(PASSES):
+                        nc.tensor.matmul_mx(
+                            out=e[:, mt - mt0, :],
+                            lhsT=v2_w[b][:, ms].bitcast(FP8X4),
+                            lhsT_scale=v2_s[4 * b : P, ms],
+                            rhs=h_w[b, half][:].bitcast(FP8X4),
+                            rhs_scale=h_s[b, half][:],
+                            start=(b == 0),
+                            stop=(b == PASSES - 1),
+                        )
+                best = outs.tile([P, PAIR, JH], F32, name="best")
+                nc.vector.tensor_tensor(best[:], e[:], sims[mt0 // 4][:, mt0 % 4 : mt0 % 4 + PAIR, js], ALU.max)
+                nc.sync.dma_start(
+                    out[P * mt0 : P * (mt0 + PAIR), js].rearrange("(mt p) j -> p mt j", p=P), best[:]
+                )
+
+        chunks = [(b, half) for half in range(HALVES) for b in range(PASSES)]
+        quantise_w1(0, 0)
+        for b, half in chunks:
+            make_size(b, half)
+        quantise_w1(0, 1)
+        quantise_w1(1, 0)
+        quantise_w1(1, 1)
+        for b, half in chunks:
+            make_recip(b, half)
+        nc.vector.tensor_copy(v2_s[:], tab_s[:].indirect(idx2[:]))
+        for a in range(PASSES):
+            nc.vector.tensor_copy(v2_w[a][:], tab_w[a][:].indirect(idx2[:]))
+        for b, half in chunks:
+            make_h(b, half)
+            if b == PASSES - 1:
+                score(half)

@@ -34,11 +34,13 @@ def tile_list_confusable_sign_scores_kernel(
         keep = ctx.enter_context(tc.tile_pool(name="keep", bufs=1))
         ring = ctx.enter_context(tc.tile_pool(name="ring", bufs=2))
         outs = ctx.enter_context(tc.tile_pool(name="outs", bufs=8))
-        psum = ctx.enter_context(tc.psum_pool(name="psum", bufs=2))
-        psum_e = ctx.enter_context(tc.psum_pool(name="psum_e", bufs=6))
+        psum = ctx.enter_context(tc.psum_pool(name="psum", bufs=1))
 
-        def held(shape, dtype, name):
-            return keep.tile(shape, dtype, name=name, align_bytes=64)
+        def held(shape, dtype, name, tag=None):
+            return keep.tile(shape, dtype, name=name, tag=tag or name, align_bytes=64)
+
+        def bank(n, name):
+            return psum.tile([P, PAIR, JH], F32, name=name, tag=f"bank{n}")
 
         idx = held([P, S // 16], U16, "idx")
         idx2 = held([P, S2 // 16], U16, "idx2")
@@ -61,9 +63,20 @@ def tile_list_confusable_sign_scores_kernel(
         nc.gpsimd.memset(w4s_raw[:].rearrange("p a c -> p (a c)").bitcast(I32), 0)
         nc.vector.memset(v_s1[:].bitcast(I32), 0)
 
+        warm_in = held([P, 1], F32, "warm_in")
+        warm_out = held([P, 1], F32, "warm_out")
+        nc.gpsimd.memset(warm_in[:], 1.0)
+        nc.scalar.activation(warm_out[:], warm_in[:], ACT.Abs_reciprocal_sqrt, bias=1.0)
+
         def load_w1(b, a):
             rows = w1[PASS * a : PASS * (a + 1), PASS * b : PASS * (b + 1)]
-            nc.sync.dma_start(w1_raw[b, a][:], rows.rearrange("(p i) c -> p i c", i=PACK))
+            rows = rows.rearrange("(p i) c -> p i c", i=PACK)
+            step = PACK // 2 if (b, a) == (0, 0) else PACK
+            for i in range(0, PACK, step):
+                nc.sync.dma_start(w1_raw[b, a][:, i : i + step, :], rows[:, i : i + step, :])
+
+        def load_tab(a):
+            nc.sync.dma_start(tab_w[a][:].bitcast(I32), tab_words[a].rearrange("p t i -> p (t i)").bitcast(I32))
 
         def load_w4_scales(q):
             nc.sync.dma_start(
@@ -79,11 +92,11 @@ def tile_list_confusable_sign_scores_kernel(
         nc.sync.dma_start(idx2[:], offs2)
         nc.sync.dma_start(gains[:], gain.rearrange("(b p t) -> p b t", p=P, t=PACK))
         nc.sync.dma_start(w4_raw[:].bitcast(I32), w4_words.rearrange("a p c -> p a c").bitcast(I32))
-        load_w1(0, 0)
+        load_tab(0)
         for q in range(QUADS):
             load_w4_scales(q)
-        for a in range(PASSES):
-            nc.sync.dma_start(tab_w[a][:].bitcast(I32), tab_words[a].rearrange("p t i -> p (t i)").bitcast(I32))
+        load_w1(0, 0)
+        load_tab(1)
 
         for b in range(PASSES):
             cols = slice(PASS * b, PASS * (b + 1))
@@ -116,25 +129,33 @@ def tile_list_confusable_sign_scores_kernel(
         w1_w, w1_s, h_w, h_s = {}, {}, {}, {}
 
         def quantise_w1(b, a):
-            rounded = ring.tile([P, PACK * PASS], BF16, name="w1_bf16", align_bytes=64)
-            dst = rounded[:].rearrange("p (t m i) -> p m i t", t=PACK, i=PACK)
-            src = w1_raw[b, a][:].rearrange("p i (m t) -> p m i t", t=PACK)
-            if (b, a) == (0, 0):
-                nc.scalar.copy(dst, src)
-            else:
-                nc.vector.tensor_copy(dst, src)
+            rounded = held([P, PACK, PASS], BF16, f"w1_bf16{b}{a}")
             w1_w[b, a] = held([P, PASS], U32, f"w1_w{b}{a}")
             w1_s[b, a] = held([P, PASS], U8, f"w1_s{b}{a}")
-            nc.vector.quantize_mx(out=w1_w[b, a][:].bitcast(FP8X4), scales=w1_s[b, a][:], in_=rounded[:])
+            for ts in pairs:
+                dst = rounded[:, ts, :].rearrange("p t (m i) -> p m i t", i=PACK)
+                src = w1_raw[b, a][:].rearrange("p i (m t) -> p m i t", t=PACK)[:, :, :, ts]
+                if a == b:
+                    nc.scalar.copy(dst, src)
+                else:
+                    nc.vector.tensor_copy(dst, src)
+            for ts in pairs:
+                cols = slice(P * ts.start, P * ts.stop)
+                nc.vector.quantize_mx(
+                    out=w1_w[b, a][:, cols].bitcast(FP8X4),
+                    scales=w1_s[b, a][:, cols],
+                    in_=rounded[:, ts, :].rearrange("p t c -> p (t c)"),
+                )
 
         pairs = [slice(PAIR * u, PAIR * (u + 1)) for u in range(PACK // PAIR)]
+        chunks = [(b, half) for half in range(HALVES) for b in range(PASSES)]
         size, recip = {}, {}
 
         def make_size(b, half):
             js = slice(JH * half, JH * (half + 1))
             size[b, half] = held([P, PACK, JH], F32, f"size{b}{half}")
-            for ts in pairs:
-                den = psum_e.tile([P, PAIR, JH], F32, name="den", tag="wide")
+            for u, ts in enumerate(pairs):
+                den = bank((2 * chunks.index((b, half)) + u) % 6, "den")
                 for t in range(ts.start, ts.stop):
                     for a in range(PASSES):
                         nc.tensor.matmul_mx(
@@ -158,9 +179,9 @@ def tile_list_confusable_sign_scores_kernel(
 
         def make_h(b, half):
             js = slice(JH * half, JH * (half + 1))
-            h32 = ring.tile([P, PACK, JH], F32, name="h32")
-            for ts in pairs:
-                num = psum.tile([P, PAIR, JH], F32, name="num")
+            h32 = held([P, PACK, JH], F32, f"h32{b}{half}")
+            for u, ts in enumerate(pairs):
+                num = bank(6 + u, "num")
                 for t in range(ts.start, ts.stop):
                     for a in range(PASSES):
                         nc.tensor.matmul_mx(
@@ -177,30 +198,40 @@ def tile_list_confusable_sign_scores_kernel(
                         h32[:, t, :], num[:, t - ts.start, :], gains[:, b, t : t + 1], recip[b, half][:, t, :],
                         ALU.mult, ALU.mult,
                     )
-            rounded = ring.tile([P, JH * PACK], BF16, name="h_bf16", align_bytes=64)
-            nc.vector.tensor_copy(
-                rounded[:].rearrange("p (c i t) -> p c t i", i=4, t=PACK),
-                h32[:].rearrange("p t (c i) -> p c t i", i=4),
-            )
+            rounded = held([P, JH * PACK], BF16, f"h_bf16{b}{half}")
             h_w[b, half] = held([P, JH], U32, f"h_w{b}{half}")
             h_s[b, half] = held([P, JH], U8, f"h_s{b}{half}")
-            nc.vector.quantize_mx(out=h_w[b, half][:].bitcast(FP8X4), scales=h_s[b, half][:], in_=rounded[:])
+            parts = [slice(0, JH // 2), slice(JH // 2, JH)]
+            for cs in parts:
+                dst = rounded[:, PACK * cs.start : PACK * cs.stop].rearrange("p (c i t) -> p c t i", i=4, t=PACK)
+                src = h32[:, :, cs].rearrange("p t (c i) -> p c t i", i=4)
+                if half == 0:
+                    nc.vector.tensor_copy(dst, src)
+                else:
+                    nc.scalar.copy(dst, src)
+            for cs in parts:
+                nc.vector.quantize_mx(
+                    out=h_w[b, half][:, cs].bitcast(FP8X4),
+                    scales=h_s[b, half][:, cs],
+                    in_=rounded[:, PACK * cs.start : PACK * cs.stop],
+                )
 
-        def score(half):
+        def score(half, row_pairs, banks):
             js = slice(JH * half, JH * (half + 1))
-            for mt0 in range(0, S2 // P, PAIR):
-                e = psum_e.tile([P, PAIR, JH], F32, name="e", tag="wide")
-                for mt in range(mt0, mt0 + PAIR):
-                    ms = slice(P * mt, P * (mt + 1))
-                    for b in range(PASSES):
+            for row_pair, n in zip(row_pairs, banks):
+                mt0 = PAIR * row_pair
+                e = bank(n, "e")
+                for b in range(PASSES):
+                    for mt in range(mt0, mt0 + PAIR):
+                        ms = slice(P * mt, P * (mt + 1))
                         nc.tensor.matmul_mx(
                             out=e[:, mt - mt0, :],
                             lhsT=v2_w[b][:, ms].bitcast(FP8X4),
                             lhsT_scale=v2_s[4 * b : P, ms],
                             rhs=h_w[b, half][:].bitcast(FP8X4),
                             rhs_scale=h_s[b, half][:],
-                            start=(b == 0),
-                            stop=(b == PASSES - 1),
+                            start=(b == 0 and mt == mt0),
+                            stop=(b == PASSES - 1 and mt == mt0 + PAIR - 1),
                         )
                 best = outs.tile([P, PAIR, JH], F32, name="best")
                 nc.vector.tensor_tensor(best[:], e[:], sims[mt0 // 4][:, mt0 % 4 : mt0 % 4 + PAIR, js], ALU.max)
@@ -208,19 +239,22 @@ def tile_list_confusable_sign_scores_kernel(
                     out[P * mt0 : P * (mt0 + PAIR), js].rearrange("(mt p) j -> p mt j", p=P), best[:]
                 )
 
-        chunks = [(b, half) for half in range(HALVES) for b in range(PASSES)]
         quantise_w1(0, 0)
         for b, half in chunks:
             make_size(b, half)
         quantise_w1(0, 1)
         quantise_w1(1, 0)
+        make_recip(*chunks[0])
         quantise_w1(1, 1)
-        for b, half in chunks:
+        for b, half in chunks[1:]:
             make_recip(b, half)
         nc.vector.tensor_copy(v2_s[:], tab_s[:].indirect(idx2[:]))
         for a in range(PASSES):
             nc.vector.tensor_copy(v2_w[a][:], tab_w[a][:].indirect(idx2[:]))
-        for b, half in chunks:
-            make_h(b, half)
-            if b == PASSES - 1:
-                score(half)
+        make_h(0, 0)
+        make_h(1, 0)
+        score(0, [0, 1], [2, 3])
+        make_h(0, 1)
+        make_h(1, 1)
+        score(0, [2, 3], [6, 7])
+        score(1, [0, 1, 2, 3], [4, 5, 0, 1])

from contextlib import ExitStack

import concourse.mybir as mybir

K, T, S, S2 = 1024, 2048, 512, 1024
FLOPS = 2 * (2 * K * K * S + S2 * K * S)

F32 = mybir.dt.float32
BF16 = mybir.dt.bfloat16
I32 = mybir.dt.int32
U32 = mybir.dt.uint32
U16 = mybir.dt.uint16
U8 = mybir.dt.uint8
FP8X4 = mybir.dt.float8_e4m3fn_x4
FP4X4 = mybir.dt.float4_e2m1fn_x4
ACT = mybir.ActivationFunctionType
ALU = mybir.AluOpType

P = 128
PACK = 4
PASS = P * PACK
PASSES = K // PASS
QUADS = 4
JH = 256
HALVES = S // JH
PAIR = 2


def tile_list_confusable_sign_scores_kernel(
    tc, tab_words, tab_scales, offs, offs2, w1, w4_words, w4_scales, gain, sim, out
):
    nc = tc.nc
    with ExitStack() as ctx:
        keep = ctx.enter_context(tc.tile_pool(name="keep", bufs=1))
        ring = ctx.enter_context(tc.tile_pool(name="ring", bufs=2))
        outs = ctx.enter_context(tc.tile_pool(name="outs", bufs=8))
        psum = ctx.enter_context(tc.psum_pool(name="psum", bufs=1))

        def held(shape, dtype, name, tag=None):
            return keep.tile(shape, dtype, name=name, tag=tag or name, align_bytes=64)

        def bank(n, name):
            return psum.tile([P, PAIR, JH], F32, name=name, tag=f"bank{n}")

        idx = held([P, S // 16], U16, "idx")
        idx2 = held([P, S2 // 16], U16, "idx2")
        tab_w = [held([P, T], U32, f"tab_w{a}") for a in range(PASSES)]
        tab_s = held([P, T], U8, "tab_s")
        w4_raw = held([P, PASSES, 2 * K], U8, "w4_raw")
        w4s_raw = held([P, PASSES, K], U8, "w4s_raw")
        w4_w = [held([P, PASSES, 2 * PASS], U8, f"w4_w{b}") for b in range(PASSES)]
        w4_s = [held([P, PASSES, PASS], U8, f"w4_s{b}") for b in range(PASSES)]
        gains = held([P, PASSES, PACK], F32, "gains")
        w1_raw = {(b, a): held([P, PACK, PASS], F32, f"w1_raw{b}{a}") for b in range(PASSES) for a in range(PASSES)}
        sims = [held([P, 4, S], F32, f"sims{c}") for c in range(2)]
        v_w = [held([P, S], U32, f"v_w{a}") for a in range(PASSES)]
        v_s = held([P, S], U8, "v_s")
        v_s1 = held([P, S], U8, "v_s1")
        v2_w = [held([P, S2], U32, f"v2_w{a}") for a in range(PASSES)]
        v2_s = held([P, S2], U8, "v2_s")

        nc.vector.memset(tab_s[:].bitcast(I32), 0)
        nc.gpsimd.memset(w4s_raw[:].rearrange("p a c -> p (a c)").bitcast(I32), 0)
        nc.vector.memset(v_s1[:].bitcast(I32), 0)

        warm_in = held([P, 1], F32, "warm_in")
        warm_out = held([P, 1], F32, "warm_out")
        nc.gpsimd.memset(warm_in[:], 1.0)
        nc.scalar.activation(warm_out[:], warm_in[:], ACT.Abs_reciprocal_sqrt, bias=1.0)

        def load_w1(b, a):
            rows = w1[PASS * a : PASS * (a + 1), PASS * b : PASS * (b + 1)]
            rows = rows.rearrange("(p i) c -> p i c", i=PACK)
            step = PACK // 2 if (b, a) == (0, 0) else PACK
            for i in range(0, PACK, step):
                nc.sync.dma_start(w1_raw[b, a][:, i : i + step, :], rows[:, i : i + step, :])

        def load_tab(a):
            nc.sync.dma_start(tab_w[a][:].bitcast(I32), tab_words[a].rearrange("p t i -> p (t i)").bitcast(I32))

        def load_w4_scales(q):
            nc.sync.dma_start(
                w4s_raw[32 * q : 32 * q + 4, :, :].bitcast(I32),
                w4_scales[:, 4 * q : 4 * q + 4, :].rearrange("a r c -> r a c").bitcast(I32),
            )

        nc.sync.dma_start(idx[:], offs)
        for q in range(QUADS):
            nc.sync.dma_start(
                tab_s[32 * q : 32 * q + 8, :].bitcast(I32), tab_scales[:, 4 * q : 4 * q + 4, :].bitcast(I32)
            )
        nc.sync.dma_start(idx2[:], offs2)
        nc.sync.dma_start(gains[:], gain.rearrange("(b p t) -> p b t", p=P, t=PACK))
        nc.sync.dma_start(w4_raw[:].bitcast(I32), w4_words.rearrange("a p c -> p a c").bitcast(I32))
        load_tab(0)
        for q in range(QUADS):
            load_w4_scales(q)
        load_w1(0, 0)
        load_tab(1)

        for b in range(PASSES):
            cols = slice(PASS * b, PASS * (b + 1))
            nc.scalar.copy(
                w4_w[b][:].bitcast(U16).rearrange("p a (t m) -> p a t m", t=PACK),
                w4_raw[:].bitcast(U16)[:, :, cols].rearrange("p a (m t) -> p a t m", t=PACK),
            )
            nc.vector.tensor_copy(
                w4_s[b][:].rearrange("p a (t m) -> p a t m", t=PACK),
                w4s_raw[:, :, cols].rearrange("p a (m t) -> p a t m", t=PACK),
            )

        nc.vector.tensor_copy(v_s[:], tab_s[:].indirect(idx[:]))
        for q in range(QUADS):
            nc.sync.dma_start(
                v_s1[32 * q : 32 * q + 4, :].bitcast(I32), v_s[32 * q + 4 : 32 * q + 8, :].bitcast(I32)
            )
        for a in range(PASSES):
            nc.vector.tensor_copy(v_w[a][:], tab_w[a][:].indirect(idx[:]))
        v_planes = [v_s, v_s1]

        load_w1(0, 1)
        load_w1(1, 0)
        load_w1(1, 1)
        for c in range(2):
            nc.sync.dma_start(
                sims[c][:], sim[PASS * c : PASS * (c + 1), :].rearrange("(mt p) j -> p mt j", p=P)
            )

        w1_w, w1_s, h_w, h_s = {}, {}, {}, {}

        def quantise_w1(b, a):
            rounded = held([P, PACK, PASS], BF16, f"w1_bf16{b}{a}")
            w1_w[b, a] = held([P, PASS], U32, f"w1_w{b}{a}")
            w1_s[b, a] = held([P, PASS], U8, f"w1_s{b}{a}")
            for ts in pairs:
                dst = rounded[:, ts, :].rearrange("p t (m i) -> p m i t", i=PACK)
                src = w1_raw[b, a][:].rearrange("p i (m t) -> p m i t", t=PACK)[:, :, :, ts]
                if a == b:
                    nc.scalar.copy(dst, src)
                else:
                    nc.vector.tensor_copy(dst, src)
            for ts in pairs:
                cols = slice(P * ts.start, P * ts.stop)
                nc.vector.quantize_mx(
                    out=w1_w[b, a][:, cols].bitcast(FP8X4),
                    scales=w1_s[b, a][:, cols],
                    in_=rounded[:, ts, :].rearrange("p t c -> p (t c)"),
                )

        pairs = [slice(PAIR * u, PAIR * (u + 1)) for u in range(PACK // PAIR)]
        chunks = [(b, half) for half in range(HALVES) for b in range(PASSES)]
        size, recip = {}, {}

        def make_size(b, half):
            js = slice(JH * half, JH * (half + 1))
            size[b, half] = held([P, PACK, JH], F32, f"size{b}{half}")
            for u, ts in enumerate(pairs):
                den = bank((2 * chunks.index((b, half)) + u) % 6, "den")
                for t in range(ts.start, ts.stop):
                    for a in range(PASSES):
                        nc.tensor.matmul_mx(
                            out=den[:, t - ts.start, :],
                            lhsT=w4_w[b][:, a, 2 * P * t : 2 * P * (t + 1)].bitcast(FP4X4),
                            lhsT_scale=w4_s[b][:, a, P * t : P * (t + 1)],
                            rhs=v_w[a][:, js].bitcast(FP8X4),
                            rhs_scale=v_planes[a][:, js],
                            start=(a == 0),
                            stop=(a == PASSES - 1),
                        )
                nc.scalar.activation(size[b, half][:, ts, :], den[:], ACT.Abs)

        def make_recip(b, half):
            root = ring.tile([P, PACK, JH], F32, name="root")
            recip[b, half] = held([P, PACK, JH], F32, f"recip{b}{half}")
            for ts in pairs:
                nc.scalar.activation(root[:, ts, :], size[b, half][:, ts, :], ACT.Abs_reciprocal_sqrt, bias=1.0)
            for ts in pairs:
                nc.scalar.activation(recip[b, half][:, ts, :], root[:, ts, :], ACT.Square)

        def make_h(b, half):
            js = slice(JH * half, JH * (half + 1))
            h32 = held([P, PACK, JH], F32, f"h32{b}{half}")
            for u, ts in enumerate(pairs):
                num = bank(6 + u, "num")
                for t in range(ts.start, ts.stop):
                    for a in range(PASSES):
                        nc.tensor.matmul_mx(
                            out=num[:, t - ts.start, :],
                            lhsT=w1_w[b, a][:, P * t : P * (t + 1)].bitcast(FP8X4),
                            lhsT_scale=w1_s[b, a][:, P * t : P * (t + 1)],
                            rhs=v_w[a][:, js].bitcast(FP8X4),
                            rhs_scale=v_planes[a][:, js],
                            start=(a == 0),
                            stop=(a == PASSES - 1),
                        )
                for t in range(ts.start, ts.stop):
                    nc.vector.scalar_tensor_tensor(
                        h32[:, t, :], num[:, t - ts.start, :], gains[:, b, t : t + 1], recip[b, half][:, t, :],
                        ALU.mult, ALU.mult,
                    )
            rounded = held([P, JH * PACK], BF16, f"h_bf16{b}{half}")
            h_w[b, half] = held([P, JH], U32, f"h_w{b}{half}")
            h_s[b, half] = held([P, JH], U8, f"h_s{b}{half}")
            parts = [slice(0, JH // 2), slice(JH // 2, JH)]
            for cs in parts:
                dst = rounded[:, PACK * cs.start : PACK * cs.stop].rearrange("p (c i t) -> p c t i", i=4, t=PACK)
                src = h32[:, :, cs].rearrange("p t (c i) -> p c t i", i=4)
                if half == 0:
                    nc.vector.tensor_copy(dst, src)
                else:
                    nc.scalar.copy(dst, src)
            for cs in parts:
                nc.vector.quantize_mx(
                    out=h_w[b, half][:, cs].bitcast(FP8X4),
                    scales=h_s[b, half][:, cs],
                    in_=rounded[:, PACK * cs.start : PACK * cs.stop],
                )

        def score(half, row_pairs, banks):
            js = slice(JH * half, JH * (half + 1))
            for row_pair, n in zip(row_pairs, banks):
                mt0 = PAIR * row_pair
                e = bank(n, "e")
                for b in range(PASSES):
                    for mt in range(mt0, mt0 + PAIR):
                        ms = slice(P * mt, P * (mt + 1))
                        nc.tensor.matmul_mx(
                            out=e[:, mt - mt0, :],
                            lhsT=v2_w[b][:, ms].bitcast(FP8X4),
                            lhsT_scale=v2_s[4 * b : P, ms],
                            rhs=h_w[b, half][:].bitcast(FP8X4),
                            rhs_scale=h_s[b, half][:],
                            start=(b == 0 and mt == mt0),
                            stop=(b == PASSES - 1 and mt == mt0 + PAIR - 1),
                        )
                best = outs.tile([P, PAIR, JH], F32, name="best")
                nc.vector.tensor_tensor(best[:], e[:], sims[mt0 // 4][:, mt0 % 4 : mt0 % 4 + PAIR, js], ALU.max)
                nc.sync.dma_start(
                    out[P * mt0 : P * (mt0 + PAIR), js].rearrange("(mt p) j -> p mt j", p=P), best[:]
                )

        quantise_w1(0, 0)
        for b, half in chunks:
            make_size(b, half)
        quantise_w1(0, 1)
        quantise_w1(1, 0)
        make_recip(*chunks[0])
        quantise_w1(1, 1)
        for b, half in chunks[1:]:
            make_recip(b, half)
        nc.vector.tensor_copy(v2_s[:], tab_s[:].indirect(idx2[:]))
        for a in range(PASSES):
            nc.vector.tensor_copy(v2_w[a][:], tab_w[a][:].indirect(idx2[:]))
        make_h(0, 0)
        make_h(1, 0)
        score(0, [0, 1], [2, 3])
        make_h(0, 1)
        make_h(1, 1)
        score(0, [2, 3], [6, 7])
        score(1, [0, 1, 2, 3], [4, 5, 0, 1])
